import numpy as np
import ml_dtypes


def mxq(x, axis, fmt="e4m3"):
    dtype, down = {"e4m3": (ml_dtypes.float8_e4m3fn, 7), "e5m2": (ml_dtypes.float8_e5m2, 14)}[fmt]
    v = np.moveaxis(np.asarray(x, np.float32).astype(ml_dtypes.bfloat16).astype(np.float64), axis, -1)
    blocks = v.reshape(v.shape[:-1] + (-1, 32))
    amax = np.abs(blocks).max(-1, keepdims=True)
    byte = np.maximum(np.where(amax > 0, np.frexp(amax)[1] - 1 + 127, 0) - down, 1)
    scale = np.exp2(byte - 127.0)
    codes = (blocks / scale).astype(np.float32).astype(dtype).astype(np.float64)
    return np.moveaxis((codes * scale).reshape(v.shape), -1, axis)


WIDE = False


def mx_kscale(k):
    if not WIDE:
        return np.ones(k)
    levels = np.array([10, -10, 5, -5, 0])
    if k % 512:
        return np.exp2(np.random.permutation(np.resize(levels, k // 32))).repeat(32)
    a = np.empty((k // 512, 16))
    for p in range(k // 512):
        a[p, :8] = np.random.permutation(np.resize(levels, 8))
        for g in range(8):
            far = levels[np.abs(levels - a[p, g]) >= 10]
            a[p, g + 8] = far[np.random.randint(len(far))]
    return np.exp2(a.ravel()).repeat(32)


def f64(x):
    return np.asarray(x).astype(np.float64)


def striped8(idx):
    return np.asarray(idx).reshape(8, -1, 16).transpose(0, 2, 1).reshape(128, -1).astype(np.uint16)


def unstriped8(offs):
    return offs.reshape(8, 16, -1).transpose(0, 2, 1).reshape(8, -1).astype(np.int64)


def pick8(x, idx, run):
    r = np.arange(len(x))
    return x[r[:, None], idx[r % (8 * run) // run]]


E2M1 = np.array([0.0, 0.5, 1.0, 1.5, 2.0, 3.0, 4.0, 6.0, -0.0, -0.5, -1.0, -1.5, -2.0, -3.0, -4.0, -6.0])


def pack_weight(w, fmt):
    k, n = w.shape
    w = f64(np.asarray(w, np.float32).astype(ml_dtypes.bfloat16)).reshape(k // 32, 32, n)
    amax = np.abs(w).max(1)
    if fmt == "e4m3":
        byte = np.frexp(amax)[1] - 1 + 127 - 7
    else:
        mant, ex = np.frexp(amax / 6.0)
        byte = np.where(mant > 0.5, ex, ex - 1) + 127
    byte = np.clip(np.where(amax > 0, byte, 1), 1, 254)
    scaled = (w * np.exp2(127.0 - byte)[:, None, :]).reshape(k, n).astype(np.float32)
    by_word = np.ascontiguousarray(scaled.reshape(k // 512, 128, 4, n).transpose(0, 1, 3, 2))
    if fmt == "e4m3":
        words = by_word.astype(ml_dtypes.float8_e4m3fn).view(np.uint8)
    else:
        c = by_word.astype(ml_dtypes.float4_e2m1fn).view(np.uint8) & 0xF
        words = (c[..., 0::2] | (c[..., 1::2] << 4)).reshape(k // 512, 128, 2 * n)
    return np.ascontiguousarray(words), np.ascontiguousarray(byte.astype(np.uint8).reshape(k // 512, 16, n))


def unpack_weight(words, scales, fmt):
    g, _, n = scales.shape
    words = np.ascontiguousarray(words).reshape(g, 128, n, -1)
    if fmt == "e4m3":
        vals = words.view(ml_dtypes.float8_e4m3fn).astype(np.float64)
    else:
        nib = np.empty((g, 128, n, 4), np.uint8)
        nib[..., 0::2] = words & 0xF
        nib[..., 1::2] = words >> 4
        vals = E2M1[nib]
    vals = vals * np.repeat(np.exp2(scales.astype(np.float64) - 127.0), 8, axis=1)[..., None]
    return vals.transpose(0, 1, 3, 2).reshape(g * 512, n)


D, K, T, U, Z, I, Q = 512, 512, 1024, 1024, 1024, 512, 128


def setup_inputs():
    n = np.random.standard_normal
    idx = np.stack([np.random.permutation(T)[:I] for _ in range(8)])
    idx2 = np.stack([np.random.permutation(U)[:I] for _ in range(8)])
    idx3 = np.stack([np.random.permutation(Z)[:I] for _ in range(8)])
    idx4 = np.stack([np.random.permutation(Z)[:I] for _ in range(8)])
    idx5 = np.stack([np.random.permutation(Z)[:I] for _ in range(8)])
    fd = mx_kscale(D)
    fk = mx_kscale(K)
    wqp = pack_weight(n((D, K)) * 1.0 / np.sqrt(D) * fd[:, None] * fk, "e4m3")
    keysp = pack_weight(n((K, T)) * 1.0 / np.sqrt(K) / fk[:, None], "e4m3")
    notesp = pack_weight(n((K, U)) * 1.0 / np.sqrt(K) / fk[:, None], "e2m1")
    return {
        "states": (n((D, Q)) * 0.95 / fd[:, None]).astype(np.float32),
        "wq_words": wqp[0],
        "wq_scales": wqp[1],
        "keys_words": keysp[0],
        "keys_scales": keysp[1],
        "notes_words": notesp[0],
        "notes_scales": notesp[1],
        "lam": (np.random.uniform(0.5, 1.5, (Q, 1))).astype(np.float32),
        "offs": striped8(idx),
        "offs2": striped8(idx2),
        "offs3": striped8(idx3),
        "offs4": striped8(idx4),
        "offs5": striped8(idx5),
    }


def reference(states, wq_words, wq_scales, keys_words, keys_scales, notes_words, notes_scales, lam, offs, offs2, offs3, offs4, offs5):
    idx = unstriped8(offs)
    idx2 = unstriped8(offs2)
    idx3 = unstriped8(offs3)
    idx4 = unstriped8(offs4)
    idx5 = unstriped8(offs5)
    wqu = unpack_weight(wq_words, wq_scales, "e4m3")
    keysu = unpack_weight(keys_words, keys_scales, "e4m3")
    notesu = unpack_weight(notes_words, notes_scales, "e2m1")
    statesq = mxq(f64(states), 0, "e4m3")
    qv = wqu.T @ statesq
    qvq = mxq(qv, 0, "e4m3")
    a = qvq.T @ keysu
    b = qvq.T @ notesu
    f1 = np.zeros((Q, Z))
    f1[np.arange(Q)[:, None], idx3[np.arange(Q) % 128 // 16]] = pick8(a, idx, 16)
    f2 = np.zeros((Q, Z))
    f2[np.arange(Q)[:, None], idx4[np.arange(Q) % 128 // 16]] = pick8(b, idx2, 16)
    cc = f1 + f2 * f64(lam)
    y = pick8(cc, idx5, 16) + pick8(a, idx, 16)
    return y

@@ -1,0 +1,184 @@
+from contextlib import ExitStack
+
+import concourse.mybir as mybir
+
+D, K, T, U, Z, SLOTS, Q = 512, 512, 1024, 1024, 1024, 512, 128
+FLOPS = 2 * (D * K * Q + K * Q * T + K * Q * U)
+
+F32 = mybir.dt.float32
+BF16 = mybir.dt.bfloat16
+I32 = mybir.dt.int32
+U32 = mybir.dt.uint32
+U16 = mybir.dt.uint16
+U8 = mybir.dt.uint8
+FP8X4 = mybir.dt.float8_e4m3fn_x4
+FP4X4 = mybir.dt.float4_e2m1fn_x4
+COPY = mybir.ActivationFunctionType.Copy
+MULT = mybir.AluOpType.mult
+ADD = mybir.AluOpType.add
+
+P = 128
+PACK = 4
+BANK = 512
+HALF = SLOTS // 2
+LANES = 16
+
+
+def load_scale_rows(queues, plane, scales):
+    for quad in range(4):
+        queues[quad].dma_start(
+            out=plane[32 * quad : 32 * quad + 4, :].bitcast(I32),
+            in_=scales[0, 4 * quad : 4 * quad + 4, :].bitcast(I32),
+        )
+
+
+def tile_attend_bridged_madetwo_kernel(
+    tc, states, wq_words, wq_scales, keys_words, keys_scales, notes_words, notes_scales,
+    lam, offs, offs2, offs3, offs4, offs5, out,
+):
+    nc = tc.nc
+    with ExitStack() as ctx:
+        lists = ctx.enter_context(tc.tile_pool(name="lists", bufs=1))
+        sb = ctx.enter_context(tc.tile_pool(name="sb", bufs=1))
+        psum = ctx.enter_context(tc.psum_pool(name="psum", bufs=1))
+
+        wq_plane = sb.tile([P, K], U8, align_bytes=64)
+        keys_plane = sb.tile([P, T], U8, align_bytes=64)
+        notes_plane = sb.tile([P, U], U8, align_bytes=64)
+        nc.vector.memset(wq_plane[:].bitcast(I32), 0)
+        nc.vector.memset(notes_plane[:].bitcast(I32), 0)
+        nc.vector.memset(keys_plane[:].bitcast(I32), 0)
+
+        states_raw = sb.tile([P, PACK, Q], F32, align_bytes=64)
+        nc.sync.dma_start(out=states_raw[:], in_=states.rearrange("(p j) q -> p j q", j=PACK))
+        wq_raw = sb.tile([P, K], I32, align_bytes=64)
+        nc.sync.dma_start(out=wq_raw[:], in_=wq_words[0].rearrange("p n t -> p (n t)").bitcast(I32))
+        load_scale_rows([nc.sync, nc.sync, nc.scalar, nc.scalar], wq_plane, wq_scales)
+        notes_codes = sb.tile([P, 2 * U], U8, align_bytes=64)
+        nc.sync.dma_start(out=notes_codes[:].bitcast(I32), in_=notes_words[0].bitcast(I32))
+        load_scale_rows([nc.sync] * 4, notes_plane, notes_scales)
+        note_list = lists.tile([P, SLOTS // LANES], U16)
+        nc.sync.dma_start(note_list[:], offs2)
+        keys_codes = sb.tile([P, T], I32, align_bytes=64)
+        nc.sync.dma_start(out=keys_codes[:], in_=keys_words[0].rearrange("p n t -> p (n t)").bitcast(I32))
+        note_places = lists.tile([P, SLOTS // LANES], U16)
+        nc.sync.dma_start(note_places[:], offs4)
+        load_scale_rows([nc.sync] * 4, keys_plane, keys_scales)
+        token_list = lists.tile([P, SLOTS // LANES], U16)
+        nc.sync.dma_start(token_list[:], offs)
+        token_places = lists.tile([P, SLOTS // LANES], U16)
+        nc.sync.dma_start(token_places[:], offs3)
+        read_places = lists.tile([P, SLOTS // LANES], U16)
+        nc.sync.dma_start(read_places[:], offs5)
+        lam_col = sb.tile([P, 1], F32)
+        nc.sync.dma_start(out=lam_col[:], in_=lam)
+
+        f1 = sb.tile([P, Z], F32, align_bytes=64)
+        f2 = sb.tile([P, Z], F32, align_bytes=64)
+        nc.vector.memset(f1[:], 0.0)
+        nc.vector.memset(f2[:], 0.0)
+
+        states_bf = sb.tile([P, Q, PACK], BF16, align_bytes=64)
+        wq_plane_dealt = sb.tile([P, PACK, P], U8, align_bytes=64)
+        nc.vector.tensor_copy(out=wq_plane_dealt[:], in_=wq_plane[:].rearrange("p (m t) -> p t m", t=PACK))
+        nc.scalar.activation(
+            out=states_bf[:, 0 : Q // 2, :].rearrange("p (c i) j -> p c j i", i=4),
+            in_=states_raw[:, :, 0 : Q // 2].rearrange("p j (c i) -> p c j i", i=4),
+            func=COPY,
+        )
+        nc.vector.tensor_copy(
+            out=states_bf[:, Q // 2 : Q, :].rearrange("p (c i) j -> p c j i", i=4),
+            in_=states_raw[:, :, Q // 2 : Q].rearrange("p j (c i) -> p c j i", i=4),
+        )
+        states_codes = sb.tile([P, Q], U32, align_bytes=64)
+        states_plane = sb.tile([P, Q], U8, align_bytes=64)
+        nc.vector.quantize_mx(
+            out=states_codes[:].bitcast(FP8X4),
+            scales=states_plane[:],
+            in_=states_bf[:].rearrange("p q j -> p (q j)"),
+        )
+
+        wq_pairs = [sb.tile([P, 2, P], I32, name=f"wq_pair{u}", align_bytes=64) for u in range(2)]
+        wq_by_place = wq_raw[:].rearrange("p (c i t) -> p c t i", i=4, t=PACK)
+        nc.vector.tensor_copy(
+            out=wq_pairs[0][:].rearrange("p t (c i) -> p c t i", i=4), in_=wq_by_place[:, :, 0:2, :]
+        )
+        nc.scalar.copy(
+            out=wq_pairs[1][:].bitcast(U32).rearrange("p t (c i) -> p c t i", i=4),
+            in_=wq_raw[:].bitcast(U32).rearrange("p (c i t) -> p c t i", i=4, t=PACK)[:, :, 2:4, :],
+        )
+        qv_bank = psum.tile([P, PACK, Q], F32)
+        for t in range(PACK):
+            nc.tensor.matmul_mx(
+                out=qv_bank[:, t, :],
+                lhsT=wq_pairs[t // 2][:, t % 2, :].bitcast(FP8X4),
+                lhsT_scale=wq_plane_dealt[:, t, :],
+                rhs=states_codes[:].bitcast(FP8X4),
+                rhs_scale=states_plane[:],
+                start=True,
+                stop=True,
+            )
+        qv_bf = sb.tile([P, Q, PACK], BF16, align_bytes=64)
+        nc.scalar.copy(out=qv_bf[:], in_=qv_bank[:].rearrange("p t q -> p q t"))
+        qv_codes = sb.tile([P, Q], U32, align_bytes=64)
+        qv_plane = sb.tile([P, Q], U8, align_bytes=64)
+        nc.vector.quantize_mx(
+            out=qv_codes[:].bitcast(FP8X4),
+            scales=qv_plane[:],
+            in_=qv_bf[:].rearrange("p q t -> p (q t)"),
+        )
+
+        a_sb = sb.tile([P, T], F32, align_bytes=64)
+        b_sb = sb.tile([P, U], F32, align_bytes=64)
+        for j in range(4):
+            cols = slice(j * HALF, (j + 1) * HALF)
+            bank = psum.tile([P, BANK], F32, name="bank", tag=f"bank{j}")
+            nc.tensor.matmul_mx(
+                out=bank[:, 0:HALF],
+                lhsT=qv_codes[:].bitcast(FP8X4),
+                lhsT_scale=qv_plane[:],
+                rhs=notes_codes[:, 2 * j * HALF : 2 * (j + 1) * HALF].bitcast(FP4X4),
+                rhs_scale=notes_plane[:, cols],
+                start=True,
+                stop=True,
+            )
+            if j % 2 == 1:
+                nc.scalar.copy(out=b_sb[:, cols], in_=bank[:, 0:HALF])
+            else:
+                nc.vector.tensor_copy(out=b_sb[:, cols], in_=bank[:, 0:HALF])
+        a_banks = [psum.tile([P, BANK], F32, name="bank", tag=f"bank{3 - h}") for h in range(2)]
+        for h in range(2):
+            cols = slice(h * BANK, (h + 1) * BANK)
+            nc.tensor.matmul_mx(
+                out=a_banks[h][:],
+                lhsT=qv_codes[:].bitcast(FP8X4),
+                lhsT_scale=qv_plane[:],
+                rhs=keys_codes[:, cols].bitcast(FP8X4),
+                rhs_scale=keys_plane[:, cols],
+                start=True,
+                stop=True,
+            )
+
+        half_cols = [slice(h * HALF // LANES, (h + 1) * HALF // LANES) for h in range(2)]
+        a_picked = sb.tile([P, SLOTS], F32, align_bytes=64)
+        b_picked = sb.tile([P, SLOTS], F32, align_bytes=64)
+        nc.vector.tensor_copy(out=b_picked[:, 0:HALF], in_=b_sb[:].indirect(note_list[:, half_cols[0]]))
+        nc.scalar.activation(out=b_picked[:, HALF:SLOTS], in_=b_sb[:].indirect(note_list[:, half_cols[1]]), func=COPY)
+        for h in range(2):
+            nc.scalar.copy(out=a_sb[:, h * BANK : (h + 1) * BANK], in_=a_banks[h][:])
+        nc.scalar.activation(out=a_picked[:], in_=a_sb[:].indirect(token_list[:]), func=COPY)
+        nc.vector.tensor_copy(out=f2[:].indirect(note_places[:]), in_=b_picked[:])
+        nc.vector.tensor_copy(out=f1[:].indirect(token_places[:]), in_=a_picked[:])
+
+        cc = sb.tile([P, Z], F32, align_bytes=64)
+        nc.vector.scalar_tensor_tensor(out=cc[:], in0=f2[:], scalar=lam_col[:], in1=f1[:], op0=MULT, op1=ADD)
+
+        result = [sb.tile([P, HALF], F32, name=f"result{h}", align_bytes=64) for h in range(2)]
+        cc_picked = sb.tile([P, HALF], F32, align_bytes=64)
+        nc.vector.tensor_tensor(
+            out=result[0][:], in0=cc[:].indirect(read_places[:, half_cols[0]]), in1=a_picked[:, 0:HALF], op=ADD
+        )
+        nc.scalar.activation(out=cc_picked[:], in_=cc[:].indirect(read_places[:, half_cols[1]]), func=COPY)
+        nc.vector.tensor_tensor(out=result[1][:], in0=cc_picked[:], in1=a_picked[:, HALF:SLOTS], op=ADD)
+        nc.sync.dma_start(out=out[:, 0:HALF], in_=result[0][:])
+        nc.scalar.dma_start(out=out[:, HALF:SLOTS], in_=result[1][:])

@@ -45,24 +45,28 @@ def tile_attend_bridged_madetwo_kernel(
         wq_plane = sb.tile([P, K], U8, align_bytes=64)
         keys_plane = sb.tile([P, T], U8, align_bytes=64)
         notes_plane = sb.tile([P, U], U8, align_bytes=64)
-        nc.vector.memset(wq_plane[:].bitcast(I32), 0)
         nc.vector.memset(notes_plane[:].bitcast(I32), 0)
         nc.vector.memset(keys_plane[:].bitcast(I32), 0)
 
+        for quad in range(4):
+            rows = wq_scales[0, 4 * quad : 4 * quad + 4, :].bitcast(I32)
+            nc.scalar.dma_start(
+                out=wq_plane[32 * quad : 32 * quad + 32, :].bitcast(I32),
+                in_=rows.unsqueeze(0).to_broadcast([8, 4, K // 4]),
+            )
         states_raw = sb.tile([P, PACK, Q], F32, align_bytes=64)
         nc.sync.dma_start(out=states_raw[:], in_=states.rearrange("(p j) q -> p j q", j=PACK))
-        wq_raw = sb.tile([P, K], I32, align_bytes=64)
+        wq_raw = sb.tile([P, K], I32, tag="wq_raw_then_f1", align_bytes=64)
         nc.sync.dma_start(out=wq_raw[:], in_=wq_words[0].rearrange("p n t -> p (n t)").bitcast(I32))
-        load_scale_rows([nc.sync, nc.sync, nc.scalar, nc.scalar], wq_plane, wq_scales)
+        note_list = lists.tile([P, SLOTS // LANES], U16)
+        nc.sync.dma_start(note_list[:], offs2)
+        note_places = lists.tile([P, SLOTS // LANES], U16)
+        nc.sync.dma_start(note_places[:], offs4)
         notes_codes = sb.tile([P, 2 * U], U8, align_bytes=64)
         nc.sync.dma_start(out=notes_codes[:].bitcast(I32), in_=notes_words[0].bitcast(I32))
         load_scale_rows([nc.sync] * 4, notes_plane, notes_scales)
-        note_list = lists.tile([P, SLOTS // LANES], U16)
-        nc.sync.dma_start(note_list[:], offs2)
         keys_codes = sb.tile([P, T], I32, align_bytes=64)
         nc.sync.dma_start(out=keys_codes[:], in_=keys_words[0].rearrange("p n t -> p (n t)").bitcast(I32))
-        note_places = lists.tile([P, SLOTS // LANES], U16)
-        nc.sync.dma_start(note_places[:], offs4)
         load_scale_rows([nc.sync] * 4, keys_plane, keys_scales)
         token_list = lists.tile([P, SLOTS // LANES], U16)
         nc.sync.dma_start(token_list[:], offs)
@@ -73,9 +77,7 @@ def tile_attend_bridged_madetwo_kernel(
         lam_col = sb.tile([P, 1], F32)
         nc.sync.dma_start(out=lam_col[:], in_=lam)
 
-        f1 = sb.tile([P, Z], F32, align_bytes=64)
         f2 = sb.tile([P, Z], F32, align_bytes=64)
-        nc.vector.memset(f1[:], 0.0)
         nc.vector.memset(f2[:], 0.0)
 
         states_bf = sb.tile([P, Q, PACK], BF16, align_bytes=64)
@@ -101,12 +103,14 @@ def tile_attend_bridged_madetwo_kernel(
         wq_pairs = [sb.tile([P, 2, P], I32, name=f"wq_pair{u}", align_bytes=64) for u in range(2)]
         wq_by_place = wq_raw[:].rearrange("p (c i t) -> p c t i", i=4, t=PACK)
         nc.vector.tensor_copy(
-            out=wq_pairs[0][:].rearrange("p t (c i) -> p c t i", i=4), in_=wq_by_place[:, :, 0:2, :]
+            out=wq_pairs[1][:].rearrange("p t (c i) -> p c t i", i=4), in_=wq_by_place[:, :, 2:4, :]
         )
         nc.scalar.copy(
-            out=wq_pairs[1][:].bitcast(U32).rearrange("p t (c i) -> p c t i", i=4),
-            in_=wq_raw[:].bitcast(U32).rearrange("p (c i t) -> p c t i", i=4, t=PACK)[:, :, 2:4, :],
+            out=wq_pairs[0][:].bitcast(U32).rearrange("p t (c i) -> p c t i", i=4),
+            in_=wq_raw[:].bitcast(U32).rearrange("p (c i t) -> p c t i", i=4, t=PACK)[:, :, 0:2, :],
         )
+        f1 = sb.tile([P, Z], F32, tag="wq_raw_then_f1", align_bytes=64)
+        nc.vector.memset(f1[:], 0.0)
         qv_bank = psum.tile([P, PACK, Q], F32)
         for t in range(PACK):
             nc.tensor.matmul_mx(
@@ -130,23 +134,25 @@ def tile_attend_bridged_madetwo_kernel(
 
         a_sb = sb.tile([P, T], F32, align_bytes=64)
         b_sb = sb.tile([P, U], F32, align_bytes=64)
-        for j in range(4):
-            cols = slice(j * HALF, (j + 1) * HALF)
+        edges = [0, 256, 512, 768, 896, 1024]
+        for j in range(5):
+            cols = slice(edges[j], edges[j + 1])
+            width = edges[j + 1] - edges[j]
             bank = psum.tile([P, BANK], F32, name="bank", tag=f"bank{j}")
             nc.tensor.matmul_mx(
-                out=bank[:, 0:HALF],
+                out=bank[:, 0:width],
                 lhsT=qv_codes[:].bitcast(FP8X4),
                 lhsT_scale=qv_plane[:],
-                rhs=notes_codes[:, 2 * j * HALF : 2 * (j + 1) * HALF].bitcast(FP4X4),
+                rhs=notes_codes[:, 2 * edges[j] : 2 * edges[j + 1]].bitcast(FP4X4),
                 rhs_scale=notes_plane[:, cols],
                 start=True,
                 stop=True,
             )
             if j % 2 == 1:
-                nc.scalar.copy(out=b_sb[:, cols], in_=bank[:, 0:HALF])
+                nc.scalar.copy(out=b_sb[:, cols], in_=bank[:, 0:width])
             else:
-                nc.vector.tensor_copy(out=b_sb[:, cols], in_=bank[:, 0:HALF])
-        a_banks = [psum.tile([P, BANK], F32, name="bank", tag=f"bank{3 - h}") for h in range(2)]
+                nc.vector.tensor_copy(out=b_sb[:, cols], in_=bank[:, 0:width])
+        a_banks = [psum.tile([P, BANK], F32, name="bank", tag=f"bank{4 - h}") for h in range(2)]
         for h in range(2):
             cols = slice(h * BANK, (h + 1) * BANK)
             nc.tensor.matmul_mx(

@@ -1,6 +1,7 @@
 from contextlib import ExitStack
 
 import concourse.mybir as mybir
+from concourse.masks import make_identity
 
 D, K, T, U, Z, SLOTS, Q = 512, 512, 1024, 1024, 1024, 512, 128
 FLOPS = 2 * (D * K * Q + K * Q * T + K * Q * U)
@@ -77,6 +78,8 @@ def tile_attend_bridged_madetwo_kernel(
         lam_col = sb.tile([P, 1], F32)
         nc.sync.dma_start(out=lam_col[:], in_=lam)
 
+        identity = sb.tile([P, P], F32, align_bytes=64)
+        make_identity(nc, identity[:])
         f2 = sb.tile([P, Z], F32, align_bytes=64)
         nc.vector.memset(f2[:], 0.0)
 
@@ -123,16 +126,18 @@ def tile_attend_bridged_madetwo_kernel(
                 stop=True,
             )
         qv_bf = sb.tile([P, Q, PACK], BF16, align_bytes=64)
-        nc.scalar.copy(out=qv_bf[:], in_=qv_bank[:].rearrange("p t q -> p q t"))
         qv_codes = sb.tile([P, Q], U32, align_bytes=64)
         qv_plane = sb.tile([P, Q], U8, align_bytes=64)
-        nc.vector.quantize_mx(
-            out=qv_codes[:].bitcast(FP8X4),
-            scales=qv_plane[:],
-            in_=qv_bf[:].rearrange("p q t -> p (q t)"),
-        )
+        for h in range(2):
+            rows = slice(h * Q // 2, (h + 1) * Q // 2)
+            nc.scalar.copy(out=qv_bf[:, rows, :], in_=qv_bank[:, :, rows].rearrange("p t q -> p q t"))
+            nc.vector.quantize_mx(
+                out=qv_codes[:, rows].bitcast(FP8X4),
+                scales=qv_plane[:, rows],
+                in_=qv_bf[:, rows, :].rearrange("p q t -> p (q t)"),
+            )
 
-        a_sb = sb.tile([P, T], F32, align_bytes=64)
+        a_sb = sb.tile([P, T], F32, tag="a_then_f2_work", align_bytes=64)
         b_sb = sb.tile([P, U], F32, align_bytes=64)
         edges = [0, 256, 512, 768, 896, 1024]
         for j in range(5):
@@ -177,7 +182,24 @@ def tile_attend_bridged_madetwo_kernel(
         nc.vector.tensor_copy(out=f1[:].indirect(token_places[:]), in_=a_picked[:])
 
         cc = sb.tile([P, Z], F32, align_bytes=64)
-        nc.vector.scalar_tensor_tensor(out=cc[:], in0=f2[:], scalar=lam_col[:], in1=f1[:], op0=MULT, op1=ADD)
+        split = 5 * P
+        f2_work = sb.tile([P, Z], F32, tag="a_then_f2_work", align_bytes=64)
+        nc.scalar.activation(out=f2_work[:, split:Z], in_=f2[:, split:Z], func=COPY, scale=lam_col[:])
+        runs = [(0, 3), (3, 5)]
+        for r, (first, last) in enumerate(runs):
+            bank = psum.tile([P, BANK], F32, name="bank", tag=f"bank{4 - r}")
+            for j in range(first, last):
+                nc.tensor.transpose(bank[:, (j - first) * P : (j - first + 1) * P], f2[:, j * P : (j + 1) * P], identity[:])
+            nc.scalar.copy(out=f2_work[:, first * P : last * P], in_=bank[:, 0 : (last - first) * P])
+        for r, (first, last) in enumerate(runs):
+            bank = psum.tile([P, BANK], F32, name="bank", tag=f"back{r}")
+            for j in range(last - first):
+                nc.tensor.transpose(bank[:, j * P : (j + 1) * P], f2_work[:, (first + j) * P : (first + j + 1) * P], identity[:])
+            cols = slice(first * P, last * P)
+            nc.vector.scalar_tensor_tensor(
+                out=cc[:, cols], in0=bank[:, 0 : (last - first) * P], scalar=lam_col[:], in1=f1[:, cols], op0=MULT, op1=ADD
+            )
+        nc.gpsimd.tensor_tensor(out=cc[:, split:Z], in0=f2_work[:, split:Z], in1=f1[:, split:Z], op=ADD)
 
         result = [sb.tile([P, HALF], F32, name=f"result{h}", align_bytes=64) for h in range(2)]
         cc_picked = sb.tile([P, HALF], F32, align_bytes=64)
@@ -186,5 +208,5 @@ def tile_attend_bridged_madetwo_kernel(
         )
         nc.scalar.activation(out=cc_picked[:], in_=cc[:].indirect(read_places[:, half_cols[1]]), func=COPY)
         nc.vector.tensor_tensor(out=result[1][:], in0=cc_picked[:], in1=a_picked[:, HALF:SLOTS], op=ADD)
-        nc.sync.dma_start(out=out[:, 0:HALF], in_=result[0][:])
-        nc.scalar.dma_start(out=out[:, HALF:SLOTS], in_=result[1][:])
+        nc.scalar.dma_start(out=out[:, 0:HALF], in_=result[0][:])
+        nc.sync.dma_start(out=out[:, HALF:SLOTS], in_=result[1][:])

from contextlib import ExitStack

import concourse.mybir as mybir
from concourse.masks import make_identity

D, K, T, U, Z, SLOTS, Q = 512, 512, 1024, 1024, 1024, 512, 128
FLOPS = 2 * (D * K * Q + K * Q * T + K * Q * U)

F32 = mybir.dt.float32
BF16 = mybir.dt.bfloat16
I32 = mybir.dt.int32
U32 = mybir.dt.uint32
U16 = mybir.dt.uint16
U8 = mybir.dt.uint8
FP8X4 = mybir.dt.float8_e4m3fn_x4
FP4X4 = mybir.dt.float4_e2m1fn_x4
COPY = mybir.ActivationFunctionType.Copy
MULT = mybir.AluOpType.mult
ADD = mybir.AluOpType.add

P = 128
PACK = 4
BANK = 512
HALF = SLOTS // 2
LANES = 16


def load_scale_rows(queues, plane, scales):
    for quad in range(4):
        queues[quad].dma_start(
            out=plane[32 * quad : 32 * quad + 4, :].bitcast(I32),
            in_=scales[0, 4 * quad : 4 * quad + 4, :].bitcast(I32),
        )


def tile_attend_bridged_madetwo_kernel(
    tc, states, wq_words, wq_scales, keys_words, keys_scales, notes_words, notes_scales,
    lam, offs, offs2, offs3, offs4, offs5, out,
):
    nc = tc.nc
    with ExitStack() as ctx:
        lists = ctx.enter_context(tc.tile_pool(name="lists", bufs=1))
        sb = ctx.enter_context(tc.tile_pool(name="sb", bufs=1))
        psum = ctx.enter_context(tc.psum_pool(name="psum", bufs=1))

        wq_plane = sb.tile([P, K], U8, align_bytes=64)
        keys_plane = sb.tile([P, T], U8, align_bytes=64)
        notes_plane = sb.tile([P, U], U8, align_bytes=64)
        nc.vector.memset(notes_plane[:].bitcast(I32), 0)
        nc.vector.memset(keys_plane[:].bitcast(I32), 0)

        for quad in range(4):
            rows = wq_scales[0, 4 * quad : 4 * quad + 4, :].bitcast(I32)
            nc.scalar.dma_start(
                out=wq_plane[32 * quad : 32 * quad + 32, :].bitcast(I32),
                in_=rows.unsqueeze(0).to_broadcast([8, 4, K // 4]),
            )
        states_raw = sb.tile([P, PACK, Q], F32, align_bytes=64)
        nc.sync.dma_start(out=states_raw[:], in_=states.rearrange("(p j) q -> p j q", j=PACK))
        wq_raw = sb.tile([P, K], I32, tag="wq_raw_then_f1", align_bytes=64)
        nc.sync.dma_start(out=wq_raw[:], in_=wq_words[0].rearrange("p n t -> p (n t)").bitcast(I32))
        note_list = lists.tile([P, SLOTS // LANES], U16)
        nc.sync.dma_start(note_list[:], offs2)
        note_places = lists.tile([P, SLOTS // LANES], U16)
        nc.sync.dma_start(note_places[:], offs4)
        notes_codes = sb.tile([P, 2 * U], U8, align_bytes=64)
        nc.sync.dma_start(out=notes_codes[:].bitcast(I32), in_=notes_words[0].bitcast(I32))
        load_scale_rows([nc.sync] * 4, notes_plane, notes_scales)
        keys_codes = sb.tile([P, T], I32, align_bytes=64)
        nc.sync.dma_start(out=keys_codes[:], in_=keys_words[0].rearrange("p n t -> p (n t)").bitcast(I32))
        load_scale_rows([nc.sync] * 4, keys_plane, keys_scales)
        token_list = lists.tile([P, SLOTS // LANES], U16)
        nc.sync.dma_start(token_list[:], offs)
        token_places = lists.tile([P, SLOTS // LANES], U16)
        nc.sync.dma_start(token_places[:], offs3)
        read_places = lists.tile([P, SLOTS // LANES], U16)
        nc.sync.dma_start(read_places[:], offs5)
        lam_col = sb.tile([P, 1], F32)
        nc.sync.dma_start(out=lam_col[:], in_=lam)

        identity = sb.tile([P, P], F32, align_bytes=64)
        make_identity(nc, identity[:])
        f2 = sb.tile([P, Z], F32, align_bytes=64)
        nc.vector.memset(f2[:], 0.0)

        states_bf = sb.tile([P, Q, PACK], BF16, align_bytes=64)
        wq_plane_dealt = sb.tile([P, PACK, P], U8, align_bytes=64)
        nc.vector.tensor_copy(out=wq_plane_dealt[:], in_=wq_plane[:].rearrange("p (m t) -> p t m", t=PACK))
        nc.scalar.activation(
            out=states_bf[:, 0 : Q // 2, :].rearrange("p (c i) j -> p c j i", i=4),
            in_=states_raw[:, :, 0 : Q // 2].rearrange("p j (c i) -> p c j i", i=4),
            func=COPY,
        )
        nc.vector.tensor_copy(
            out=states_bf[:, Q // 2 : Q, :].rearrange("p (c i) j -> p c j i", i=4),
            in_=states_raw[:, :, Q // 2 : Q].rearrange("p j (c i) -> p c j i", i=4),
        )
        states_codes = sb.tile([P, Q], U32, align_bytes=64)
        states_plane = sb.tile([P, Q], U8, align_bytes=64)
        nc.vector.quantize_mx(
            out=states_codes[:].bitcast(FP8X4),
            scales=states_plane[:],
            in_=states_bf[:].rearrange("p q j -> p (q j)"),
        )

        wq_pairs = [sb.tile([P, 2, P], I32, name=f"wq_pair{u}", align_bytes=64) for u in range(2)]
        wq_by_place = wq_raw[:].rearrange("p (c i t) -> p c t i", i=4, t=PACK)
        nc.vector.tensor_copy(
            out=wq_pairs[1][:].rearrange("p t (c i) -> p c t i", i=4), in_=wq_by_place[:, :, 2:4, :]
        )
        nc.scalar.copy(
            out=wq_pairs[0][:].bitcast(U32).rearrange("p t (c i) -> p c t i", i=4),
            in_=wq_raw[:].bitcast(U32).rearrange("p (c i t) -> p c t i", i=4, t=PACK)[:, :, 0:2, :],
        )
        f1 = sb.tile([P, Z], F32, tag="wq_raw_then_f1", align_bytes=64)
        nc.vector.memset(f1[:], 0.0)
        qv_bank = psum.tile([P, PACK, Q], F32)
        for t in range(PACK):
            nc.tensor.matmul_mx(
                out=qv_bank[:, t, :],
                lhsT=wq_pairs[t // 2][:, t % 2, :].bitcast(FP8X4),
                lhsT_scale=wq_plane_dealt[:, t, :],
                rhs=states_codes[:].bitcast(FP8X4),
                rhs_scale=states_plane[:],
                start=True,
                stop=True,
            )
        qv_bf = sb.tile([P, Q, PACK], BF16, align_bytes=64)
        qv_codes = sb.tile([P, Q], U32, align_bytes=64)
        qv_plane = sb.tile([P, Q], U8, align_bytes=64)
        for h in range(2):
            rows = slice(h * Q // 2, (h + 1) * Q // 2)
            nc.scalar.copy(out=qv_bf[:, rows, :], in_=qv_bank[:, :, rows].rearrange("p t q -> p q t"))
            nc.vector.quantize_mx(
                out=qv_codes[:, rows].bitcast(FP8X4),
                scales=qv_plane[:, rows],
                in_=qv_bf[:, rows, :].rearrange("p q t -> p (q t)"),
            )

        a_sb = sb.tile([P, T], F32, tag="a_then_f2_work", align_bytes=64)
        b_sb = sb.tile([P, U], F32, align_bytes=64)
        edges = [0, 256, 512, 768, 896, 1024]
        for j in range(5):
            cols = slice(edges[j], edges[j + 1])
            width = edges[j + 1] - edges[j]
            bank = psum.tile([P, BANK], F32, name="bank", tag=f"bank{j}")
            nc.tensor.matmul_mx(
                out=bank[:, 0:width],
                lhsT=qv_codes[:].bitcast(FP8X4),
                lhsT_scale=qv_plane[:],
                rhs=notes_codes[:, 2 * edges[j] : 2 * edges[j + 1]].bitcast(FP4X4),
                rhs_scale=notes_plane[:, cols],
                start=True,
                stop=True,
            )
            if j % 2 == 1:
                nc.scalar.copy(out=b_sb[:, cols], in_=bank[:, 0:width])
            else:
                nc.vector.tensor_copy(out=b_sb[:, cols], in_=bank[:, 0:width])
        a_banks = [psum.tile([P, BANK], F32, name="bank", tag=f"bank{4 - h}") for h in range(2)]
        for h in range(2):
            cols = slice(h * BANK, (h + 1) * BANK)
            nc.tensor.matmul_mx(
                out=a_banks[h][:],
                lhsT=qv_codes[:].bitcast(FP8X4),
                lhsT_scale=qv_plane[:],
                rhs=keys_codes[:, cols].bitcast(FP8X4),
                rhs_scale=keys_plane[:, cols],
                start=True,
                stop=True,
            )

        half_cols = [slice(h * HALF // LANES, (h + 1) * HALF // LANES) for h in range(2)]
        a_picked = sb.tile([P, SLOTS], F32, align_bytes=64)
        b_picked = sb.tile([P, SLOTS], F32, align_bytes=64)
        nc.vector.tensor_copy(out=b_picked[:, 0:HALF], in_=b_sb[:].indirect(note_list[:, half_cols[0]]))
        nc.scalar.activation(out=b_picked[:, HALF:SLOTS], in_=b_sb[:].indirect(note_list[:, half_cols[1]]), func=COPY)
        for h in range(2):
            nc.scalar.copy(out=a_sb[:, h * BANK : (h + 1) * BANK], in_=a_banks[h][:])
        nc.scalar.activation(out=a_picked[:], in_=a_sb[:].indirect(token_list[:]), func=COPY)
        nc.vector.tensor_copy(out=f2[:].indirect(note_places[:]), in_=b_picked[:])
        nc.vector.tensor_copy(out=f1[:].indirect(token_places[:]), in_=a_picked[:])

        cc = sb.tile([P, Z], F32, align_bytes=64)
        split = 5 * P
        f2_work = sb.tile([P, Z], F32, tag="a_then_f2_work", align_bytes=64)
        nc.scalar.activation(out=f2_work[:, split:Z], in_=f2[:, split:Z], func=COPY, scale=lam_col[:])
        runs = [(0, 3), (3, 5)]
        for r, (first, last) in enumerate(runs):
            bank = psum.tile([P, BANK], F32, name="bank", tag=f"bank{4 - r}")
            for j in range(first, last):
                nc.tensor.transpose(bank[:, (j - first) * P : (j - first + 1) * P], f2[:, j * P : (j + 1) * P], identity[:])
            nc.scalar.copy(out=f2_work[:, first * P : last * P], in_=bank[:, 0 : (last - first) * P])
        for r, (first, last) in enumerate(runs):
            bank = psum.tile([P, BANK], F32, name="bank", tag=f"back{r}")
            for j in range(last - first):
                nc.tensor.transpose(bank[:, j * P : (j + 1) * P], f2_work[:, (first + j) * P : (first + j + 1) * P], identity[:])
            cols = slice(first * P, last * P)
            nc.vector.scalar_tensor_tensor(
                out=cc[:, cols], in0=bank[:, 0 : (last - first) * P], scalar=lam_col[:], in1=f1[:, cols], op0=MULT, op1=ADD
            )
        nc.gpsimd.tensor_tensor(out=cc[:, split:Z], in0=f2_work[:, split:Z], in1=f1[:, split:Z], op=ADD)

        result = [sb.tile([P, HALF], F32, name=f"result{h}", align_bytes=64) for h in range(2)]
        cc_picked = sb.tile([P, HALF], F32, align_bytes=64)
        nc.vector.tensor_tensor(
            out=result[0][:], in0=cc[:].indirect(read_places[:, half_cols[0]]), in1=a_picked[:, 0:HALF], op=ADD
        )
        nc.scalar.activation(out=cc_picked[:], in_=cc[:].indirect(read_places[:, half_cols[1]]), func=COPY)
        nc.vector.tensor_tensor(out=result[1][:], in0=cc_picked[:], in1=a_picked[:, HALF:SLOTS], op=ADD)
        nc.scalar.dma_start(out=out[:, 0:HALF], in_=result[0][:])
        nc.sync.dma_start(out=out[:, HALF:SLOTS], in_=result[1][:])
